import numpy as np
import ml_dtypes


def mxq(x, axis, fmt="e4m3"):
    dtype, down = {"e4m3": (ml_dtypes.float8_e4m3fn, 7), "e5m2": (ml_dtypes.float8_e5m2, 14)}[fmt]
    v = np.moveaxis(np.asarray(x, np.float32).astype(ml_dtypes.bfloat16).astype(np.float64), axis, -1)
    blocks = v.reshape(v.shape[:-1] + (-1, 32))
    amax = np.abs(blocks).max(-1, keepdims=True)
    byte = np.maximum(np.where(amax > 0, np.frexp(amax)[1] - 1 + 127, 0) - down, 1)
    scale = np.exp2(byte - 127.0)
    codes = (blocks / scale).astype(np.float32).astype(dtype).astype(np.float64)
    return np.moveaxis((codes * scale).reshape(v.shape), -1, axis)


WIDE = False


def mx_kscale(k):
    if not WIDE:
        return np.ones(k)
    levels = np.array([10, -10, 5, -5, 0])
    if k % 512:
        return np.exp2(np.random.permutation(np.resize(levels, k // 32))).repeat(32)
    a = np.empty((k // 512, 16))
    for p in range(k // 512):
        a[p, :8] = np.random.permutation(np.resize(levels, 8))
        for g in range(8):
            far = levels[np.abs(levels - a[p, g]) >= 10]
            a[p, g + 8] = far[np.random.randint(len(far))]
    return np.exp2(a.ravel()).repeat(32)


def f64(x):
    return np.asarray(x).astype(np.float64)


def striped(idx):
    return np.tile(np.asarray(idx).reshape(-1, 16).T, (8, 1)).astype(np.uint16)


def unstriped(offs):
    return offs[:16].T.reshape(-1).astype(np.int64)


E2M1 = np.array([0.0, 0.5, 1.0, 1.5, 2.0, 3.0, 4.0, 6.0, -0.0, -0.5, -1.0, -1.5, -2.0, -3.0, -4.0, -6.0])


def pack_weight(w, fmt):
    k, n = w.shape
    w = f64(np.asarray(w, np.float32).astype(ml_dtypes.bfloat16)).reshape(k // 32, 32, n)
    amax = np.abs(w).max(1)
    if fmt == "e4m3":
        byte = np.frexp(amax)[1] - 1 + 127 - 7
    else:
        mant, ex = np.frexp(amax / 6.0)
        byte = np.where(mant > 0.5, ex, ex - 1) + 127
    byte = np.clip(np.where(amax > 0, byte, 1), 1, 254)
    scaled = (w * np.exp2(127.0 - byte)[:, None, :]).reshape(k, n).astype(np.float32)
    by_word = np.ascontiguousarray(scaled.reshape(k // 512, 128, 4, n).transpose(0, 1, 3, 2))
    if fmt == "e4m3":
        words = by_word.astype(ml_dtypes.float8_e4m3fn).view(np.uint8)
    else:
        c = by_word.astype(ml_dtypes.float4_e2m1fn).view(np.uint8) & 0xF
        words = (c[..., 0::2] | (c[..., 1::2] << 4)).reshape(k // 512, 128, 2 * n)
    return np.ascontiguousarray(words), np.ascontiguousarray(byte.astype(np.uint8).reshape(k // 512, 16, n))


def unpack_weight(words, scales, fmt):
    g, _, n = scales.shape
    words = np.ascontiguousarray(words).reshape(g, 128, n, -1)
    if fmt == "e4m3":
        vals = words.view(ml_dtypes.float8_e4m3fn).astype(np.float64)
    else:
        nib = np.empty((g, 128, n, 4), np.uint8)
        nib[..., 0::2] = words & 0xF
        nib[..., 1::2] = words >> 4
        vals = E2M1[nib]
    vals = vals * np.repeat(np.exp2(scales.astype(np.float64) - 127.0), 8, axis=1)[..., None]
    return vals.transpose(0, 1, 3, 2).reshape(g * 512, n)


def bf(x):
    return np.asarray(x, np.float32).astype(ml_dtypes.bfloat16)


def planes(Y):
    r, m = Y.shape
    b = f64(bf(Y)).reshape(r // 32, 32, m)
    amax = np.abs(b).max(1)
    byte = np.clip(np.where(amax > 0, np.frexp(amax)[1] - 1 + 127 - 7, 1), 1, 254)
    codes = (b * np.exp2(127.0 - byte)[:, None, :]).reshape(r, m).astype(np.float32).astype(ml_dtypes.float8_e4m3fn).view(np.uint8)
    words = codes.reshape(r // 512, 128, 4, m).transpose(0, 1, 3, 2)
    return np.ascontiguousarray(words), np.ascontiguousarray(byte.astype(np.uint8).reshape(r // 512, 16, m))


D, T, I, J, U, E, Y = 512, 2048, 512, 512, 1024, 512, 1024


def setup_inputs():
    n = np.random.standard_normal
    idx = np.random.permutation(T)[:I]
    idx2 = np.random.permutation(U)[:J]
    idx3 = np.random.permutation(U)[:J]
    idx4 = np.random.permutation(Y)[:I]
    fd = mx_kscale(D)
    fi = mx_kscale(I)
    ti = np.ones(T)
    ti[idx] = fi
    ti4 = np.ones(Y)
    ti4[idx4] = fi
    keysp = pack_weight(n((D, T)) / fd[:, None], "e2m1")
    return {
        "keys_words": keysp[0],
        "keys_scales": keysp[1],
        "notes": (n((D, U)) * 1.0 / np.sqrt(D) * fd[:, None]).astype(np.float32),
        "rowf": (np.random.uniform(0.02, 0.08, (I, 1)) * fi[:, None]).astype(np.float32),
        "rowf2": (np.random.uniform(0.02, 0.08, (I, 1)) * fi[:, None]).astype(np.float32),
        "vals": (n((E, T)) / ti).astype(np.float32),
        "vals2": (n((E, Y)) / ti4).astype(np.float32),
        "offs": striped(idx),
        "offs2": striped(idx2),
        "offs3": striped(idx3),
        "offs4": striped(idx4),
    }


def reference(keys_words, keys_scales, notes, rowf, rowf2, vals, vals2, offs, offs2, offs3, offs4):
    idx = unstriped(offs)
    idx2 = unstriped(offs2)
    idx3 = unstriped(offs3)
    idx4 = unstriped(offs4)
    keysu = unpack_weight(keys_words, keys_scales, "e2m1")
    keysidxg = keysu[:, idx]
    notesq = mxq(f64(notes), 0, "e4m3")
    g1 = keysidxg.T @ notesq
    g9 = g1[:, idx2] - g1[:, idx3]
    g0 = np.maximum(g9, 0.0)
    gr1 = g0 * f64(rowf)
    gr2 = g0 * f64(rowf2)
    vt1 = f64(vals)[:, idx].T
    vt2 = f64(vals2)[:, idx4].T
    vt1q = mxq(vt1, 0, "e4m3")
    gr1q = mxq(gr1, 0, "e4m3")
    vt2q = mxq(vt2, 0, "e4m3")
    gr2q = mxq(gr2, 0, "e4m3")
    o = vt1q.T @ gr1q + vt2q.T @ gr2q
    words, scales = planes(o)
    return o, words, scales

@@ -1,0 +1,211 @@
+from contextlib import ExitStack
+
+import concourse.mybir as mybir
+from concourse.masks import make_identity
+
+F32 = mybir.dt.float32
+BF16 = mybir.dt.bfloat16
+I32 = mybir.dt.int32
+U32 = mybir.dt.uint32
+U16 = mybir.dt.uint16
+U8 = mybir.dt.uint8
+FP8X4 = mybir.dt.float8_e4m3fn_x4
+FP4X4 = mybir.dt.float4_e2m1fn_x4
+COPY = mybir.ActivationFunctionType.Copy
+ALU = mybir.AluOpType
+
+D, T, I, J, U, E, Y = 512, 2048, 512, 512, 1024, 512, 1024
+P = 128
+PACK = 4
+BANK = 512
+NOTE_HALVES = U // BANK
+CHUNKS = 2
+JC = J // CHUNKS
+SCALAR_NOTE_COLS = 256
+
+FLOPS = 2 * D * I * U + 2 * 2 * I * E * J
+
+
+def tile_attend_tab_looked_twostores_pl_kernel(
+    tc, keys_words, keys_scales, notes, rowf, rowf2, vals, vals2, offs, offs2, offs3, offs4, out_0, out_1, out_2
+):
+    nc = tc.nc
+    with ExitStack() as ctx:
+        held = ctx.enter_context(tc.tile_pool(name="held", bufs=1))
+        sums = ctx.enter_context(tc.psum_pool(name="sums", bufs=6))
+        turns = ctx.enter_context(tc.psum_pool(name="turns", bufs=2))
+
+        def sb(name, shape, dtype, tag=None):
+            return held.tile(shape, dtype, name=name, tag=tag or name, align_bytes=64)
+
+        def weave(engine_copy, dst, src):
+            engine_copy(dst.rearrange("p (c i) t -> p c t i", i=4), src.rearrange("p t (c i) -> p c t i", i=4))
+
+        def gather(engine, out, window):
+            if engine == "v":
+                nc.vector.tensor_copy(out, window)
+            else:
+                nc.scalar.activation(out, window, COPY)
+
+        lists = {}
+        for name in ("offs", "offs2", "offs3", "offs4"):
+            lists[name] = held.tile([P, I // 16], U16, name="list_" + name)
+        key_words = sb("key_words", [P, T], U16)
+        key_scales = sb("key_scales", [P, T], U8)
+        notes_raw = [sb("notes_raw%d" % h, [P, PACK, BANK], F32) for h in range(NOTE_HALVES)]
+        stores = ((vals, T, "offs"), (vals2, Y, "offs4"))
+        planes = [[sb("plane%d_%d" % (s, r), [P, stores[s][1]], F32) for r in range(PACK)] for s in range(2)]
+        factors = [sb("factor%d" % s, [P, PACK], F32) for s in range(2)]
+
+        nc.gpsimd.memset(key_scales[:].bitcast(I32), 0)
+        nc.sync.dma_start(lists["offs"][:], offs)
+        for q in range(4):
+            nc.sync.dma_start(
+                key_scales[32 * q : 32 * q + 4, :].bitcast(I32), keys_scales[0, 4 * q : 4 * q + 4, :].bitcast(I32)
+            )
+        nc.sync.dma_start(key_words[:].bitcast(I32), keys_words[0].bitcast(I32))
+        notes_rows = notes.rearrange("(p t) u -> p t u", t=PACK)
+        for h in range(NOTE_HALVES):
+            nc.sync.dma_start(notes_raw[h][:], notes_rows[:, :, h * BANK : (h + 1) * BANK])
+        nc.sync.dma_start(lists["offs4"][:], offs4)
+        nc.sync.dma_start(lists["offs3"][:], offs3)
+        nc.sync.dma_start(lists["offs2"][:], offs2)
+        for s, factor in enumerate((rowf, rowf2)):
+            nc.sync.dma_start(factors[s][:], factor.rearrange("(p t) o -> p (t o)", t=PACK))
+        for r in range(PACK):
+            for s in range(2):
+                nc.sync.dma_start(planes[s][r][:], stores[s][0].rearrange("(p r) c -> r p c", r=PACK)[r])
+        identity = sb("identity", [P, P], F32)
+        make_identity(nc, identity[:])
+
+        picked_words = sb("picked_words", [P, I], U16)
+        dealt_words = sb("dealt_words", [P, I], U16)
+        dealt_scales = sb("dealt_scales", [P, I], U8)
+        nc.vector.tensor_copy(
+            dealt_scales[:].rearrange("p (t m) -> p m t", t=PACK), key_scales[:].indirect(lists["offs"][:])
+        )
+        nc.vector.tensor_copy(picked_words[:], key_words[:].indirect(lists["offs"][:]))
+        nc.vector.tensor_copy(
+            dealt_words[:].rearrange("p (t m) -> p t m", t=PACK), picked_words[:].rearrange("p (m t) -> p t m", t=PACK)
+        )
+
+        wide = [sb("wide%d" % t, [P, U], F32) for t in range(PACK)]
+        for h in range(NOTE_HALVES):
+            grouped = sb("notes_grouped%d" % h, [P, BANK, PACK], BF16, "notes_grouped")
+            cut = SCALAR_NOTE_COLS if h == 0 else 0
+            if cut:
+                weave(nc.scalar.copy, grouped[:, :cut, :], notes_raw[h][:, :, :cut])
+            weave(nc.vector.tensor_copy, grouped[:, cut:, :], notes_raw[h][:, :, cut:])
+            codes = sb("notes_codes%d" % h, [P, BANK], U32)
+            scales = sb("notes_scales%d" % h, [P, BANK], U8)
+            nc.vector.quantize_mx(codes[:].bitcast(FP8X4), scales[:], grouped[:].rearrange("p u t -> p (u t)"))
+            for t in range(PACK):
+                cols = slice(t * P, (t + 1) * P)
+                bank = sums.tile([P, BANK], F32, name="bank")
+                nc.tensor.matmul_mx(
+                    bank[:], lhsT=dealt_words[:, cols].bitcast(FP4X4), lhsT_scale=dealt_scales[:, cols],
+                    rhs=codes[:].bitcast(FP8X4), rhs_scale=scales[:], start=True, stop=True,
+                )
+                nc.scalar.copy(wide[t][:, h * BANK : (h + 1) * BANK], bank[:])
+
+        values_grouped = [sb("values_grouped%d" % g, [P, 2, 2 * P * PACK], BF16) for g in range(2)]
+        value_codes, value_scales = {}, {}
+
+        def values(r, engines, tags):
+            turned = turns.tile([P, 2, 2, P], F32, name="turned")
+            for s in range(2):
+                picked = sb("picked%d_%d" % (s, r), [P, I], BF16, tags[s])
+                gather(engines[s], picked[:], planes[s][r][:].indirect(lists[stores[s][2]][:]))
+                pairs = picked[:].bitcast(F32)
+                for u in range(2):
+                    nc.tensor.transpose(turned[:, s, u, :], pairs[:, u : I // 2 : 2], identity[:])
+            nc.scalar.copy(
+                values_grouped[r // 2][:, r % 2, :].bitcast(F32).rearrange("p (s e u) -> p s e u", s=2, u=2),
+                turned[:].rearrange("p s u e -> p s e u"),
+            )
+
+        def quantise_values(g, tag):
+            value_codes[g] = sb("values_codes%d" % g, [P, 4 * P], U32, tag)
+            value_scales[g] = sb("values_scales%d" % g, [P, 4 * P], U8)
+            nc.vector.quantize_mx(
+                value_codes[g][:].bitcast(FP8X4), value_scales[g][:], values_grouped[g][:].rearrange("p r x -> p (r x)")
+            )
+
+        table_codes, table_scales, seconds = {}, {}, {}
+
+        def look_up_second(c, engine):
+            entries = slice(c * JC // 16, (c + 1) * JC // 16)
+            seconds[c] = sb("second%d" % c, [P, PACK, JC], F32)
+            for t in range(PACK):
+                gather(engine, seconds[c][:, t, :], wide[t][:].indirect(lists["offs3"][:, entries]))
+
+        def table(c, raw_tag):
+            entries = slice(c * JC // 16, (c + 1) * JC // 16)
+            scaled = [sb("scaled%d_%d" % (s, c), [P, PACK, JC], BF16) for s in range(2)]
+            raw = sb("raw%d" % c, [P, PACK, JC], F32, raw_tag)
+            for t in range(PACK):
+                nc.vector.tensor_tensor(
+                    raw[:, t, :], wide[t][:].indirect(lists["offs2"][:, entries]), seconds[c][:, t, :], ALU.subtract
+                )
+            for s in range(2):
+                for t in range(PACK):
+                    nc.vector.tensor_scalar(
+                        scaled[s][:, t, :], raw[:, t, :], 0.0, factors[s][:, t : t + 1], ALU.max, ALU.mult
+                    )
+            grouped = sb("table_grouped%d" % c, [P, 2, JC, PACK], BF16)
+            for s in range(2):
+                weave(nc.vector.tensor_copy, grouped[:, s, :, :], scaled[s][:])
+            table_codes[c] = sb("table_codes%d" % c, [P, 2 * JC], U32)
+            table_scales[c] = sb("table_scales%d" % c, [P, 2 * JC], U8)
+            nc.vector.quantize_mx(
+                table_codes[c][:].bitcast(FP8X4), table_scales[c][:], grouped[:].rearrange("p s j t -> p (s j t)")
+            )
+
+        out_scales = sb("out_scales", [P, J], U8)
+        out_rows = out_0.rearrange("(p r) j -> p r j", r=PACK)
+        out_words = out_1[0].rearrange("p j t -> p (j t)").bitcast(I32)
+
+        def result(c, tag):
+            cols = slice(c * JC, (c + 1) * JC)
+            sums_sb = sb("result%d" % c, [P, PACK, JC], F32, tag)
+            per_bank = BANK // JC
+            for r0 in range(0, PACK, per_bank):
+                if r0 == 0:
+                    bank = turns.tile([P, BANK], F32, name="early_bank", tag="turned")
+                else:
+                    bank = sums.tile([P, BANK], F32, name="bank")
+                for r in range(r0, r0 + per_bank):
+                    for s in range(2):
+                        e_cols = slice((2 * (r % 2) + s) * P, (2 * (r % 2) + s + 1) * P)
+                        j_cols = slice(s * JC, (s + 1) * JC)
+                        nc.tensor.matmul_mx(
+                            bank[:, (r - r0) * JC : (r - r0 + 1) * JC],
+                            lhsT=value_codes[r // 2][:, e_cols].bitcast(FP8X4),
+                            lhsT_scale=value_scales[r // 2][:, e_cols],
+                            rhs=table_codes[c][:, j_cols].bitcast(FP8X4), rhs_scale=table_scales[c][:, j_cols],
+                            start=(s == 0), stop=(s == 1),
+                        )
+                copy_out = nc.vector.tensor_copy if (c == CHUNKS - 1 and r0 > 0) else nc.scalar.copy
+                copy_out(sums_sb[:, r0 : r0 + per_bank, :].rearrange("p r j -> p (r j)"), bank[:])
+            nc.sync.dma_start(out_rows[:, :, cols], sums_sb[:])
+            grouped = sb("result_grouped%d" % c, [P, JC, PACK], BF16)
+            weave(nc.vector.tensor_copy if c == CHUNKS - 1 else nc.scalar.copy, grouped[:], sums_sb[:])
+            codes = sb("result_codes%d" % c, [P, JC], U32)
+            nc.vector.quantize_mx(codes[:].bitcast(FP8X4), out_scales[:, cols], grouped[:].rearrange("p j r -> p (j r)"))
+            nc.sync.dma_start(out_words[:, cols], codes[:].bitcast(I32))
+
+        values(0, "vs", ("notes_grouped", "notes_codes1"))
+        look_up_second(0, "v")
+        table(0, None)
+        look_up_second(1, "s")
+        values(1, "ss", ("notes_scales1", "notes_codes1"))
+        table(1, "scaled0_0")
+        quantise_values(0, "second1")
+        values(2, "sv", ("notes_scales1", "table_grouped0"))
+        values(3, "ss", ("notes_scales1", "notes_codes1"))
+        quantise_values(1, "scaled0_1")
+        result(0, "notes_codes1")
+        result(1, None)
+        for q in range(4):
+            queue = nc.sync if q % 2 == 0 else nc.scalar
+            queue.dma_start(out_2[0, 4 * q : 4 * q + 4, :].bitcast(I32), out_scales[32 * q : 32 * q + 4, :].bitcast(I32))

@@ -19,8 +19,9 @@ P = 128
 PACK = 4
 BANK = 512
 NOTE_HALVES = U // BANK
-CHUNKS = 2
-JC = J // CHUNKS
+HALF = J // 2
+SCALAR_SECONDS = (2, 3)
+QV2_TAG = "second1_2"
 SCALAR_NOTE_COLS = 256
 
 FLOPS = 2 * D * I * U + 2 * 2 * I * E * J
@@ -33,7 +34,7 @@ def tile_attend_tab_looked_twostores_pl_kernel(
     with ExitStack() as ctx:
         held = ctx.enter_context(tc.tile_pool(name="held", bufs=1))
         sums = ctx.enter_context(tc.psum_pool(name="sums", bufs=6))
-        turns = ctx.enter_context(tc.psum_pool(name="turns", bufs=2))
+        turns = ctx.enter_context(tc.psum_pool(name="turns", bufs=1))
 
         def sb(name, shape, dtype, tag=None):
             return held.tile(shape, dtype, name=name, tag=tag or name, align_bytes=64)
@@ -108,104 +109,117 @@ def tile_attend_tab_looked_twostores_pl_kernel(
                 )
                 nc.scalar.copy(wide[t][:, h * BANK : (h + 1) * BANK], bank[:])
 
-        values_grouped = [sb("values_grouped%d" % g, [P, 2, 2 * P * PACK], BF16) for g in range(2)]
-        value_codes, value_scales = {}, {}
+        values_grouped, value_codes, value_scales = {}, {}, {}
 
         def values(r, engines, tags):
-            turned = turns.tile([P, 2, 2, P], F32, name="turned")
+            turned = turns.tile([P, 2, 2, P], F32, name="turned", tag="turned%d" % (r % 2))
             for s in range(2):
                 picked = sb("picked%d_%d" % (s, r), [P, I], BF16, tags[s])
                 gather(engines[s], picked[:], planes[s][r][:].indirect(lists[stores[s][2]][:]))
                 pairs = picked[:].bitcast(F32)
                 for u in range(2):
                     nc.tensor.transpose(turned[:, s, u, :], pairs[:, u : I // 2 : 2], identity[:])
+            return turned
+
+        def leave_bank(r, turned, tag):
+            values_grouped[r] = sb("values_grouped%d" % r, [P, 2 * P * PACK], BF16, tag)
             nc.scalar.copy(
-                values_grouped[r // 2][:, r % 2, :].bitcast(F32).rearrange("p (s e u) -> p s e u", s=2, u=2),
+                values_grouped[r][:].bitcast(F32).rearrange("p (s e u) -> p s e u", s=2, u=2),
                 turned[:].rearrange("p s u e -> p s e u"),
             )
 
-        def quantise_values(g, tag):
-            value_codes[g] = sb("values_codes%d" % g, [P, 4 * P], U32, tag)
-            value_scales[g] = sb("values_scales%d" % g, [P, 4 * P], U8)
-            nc.vector.quantize_mx(
-                value_codes[g][:].bitcast(FP8X4), value_scales[g][:], values_grouped[g][:].rearrange("p r x -> p (r x)")
-            )
+        def quantise_values(r, tag):
+            value_codes[r] = sb("values_codes%d" % r, [P, 2 * P], U32, tag)
+            value_scales[r] = sb("values_scales%d" % r, [P, 2 * P], U8)
+            nc.vector.quantize_mx(value_codes[r][:].bitcast(FP8X4), value_scales[r][:], values_grouped[r][:])
 
-        table_codes, table_scales, seconds = {}, {}, {}
+        seconds = {}
 
-        def look_up_second(c, engine):
-            entries = slice(c * JC // 16, (c + 1) * JC // 16)
-            seconds[c] = sb("second%d" % c, [P, PACK, JC], F32)
+        def look_up_second(half, t, engine, tag):
+            entries = slice(half * HALF // 16, (half + 1) * HALF // 16)
+            seconds[half, t] = sb("second%d_%d" % (half, t), [P, HALF], F32, tag)
+            gather(engine, seconds[half, t][:], wide[t][:].indirect(lists["offs3"][:, entries]))
+
+        def scaled_table(half, raw_tag, second_tags):
+            entries = slice(half * HALF // 16, (half + 1) * HALF // 16)
+            raw = sb("raw%d" % half, [P, PACK, HALF], F32, raw_tag)
+            scaled = sb("scaled%d" % half, [P, 2, PACK, HALF], BF16)
             for t in range(PACK):
-                gather(engine, seconds[c][:, t, :], wide[t][:].indirect(lists["offs3"][:, entries]))
-
-        def table(c, raw_tag):
-            entries = slice(c * JC // 16, (c + 1) * JC // 16)
-            scaled = [sb("scaled%d_%d" % (s, c), [P, PACK, JC], BF16) for s in range(2)]
-            raw = sb("raw%d" % c, [P, PACK, JC], F32, raw_tag)
-            for t in range(PACK):
+                if (half, t) not in seconds:
+                    look_up_second(half, t, "v", second_tags[t])
                 nc.vector.tensor_tensor(
-                    raw[:, t, :], wide[t][:].indirect(lists["offs2"][:, entries]), seconds[c][:, t, :], ALU.subtract
+                    raw[:, t, :], wide[t][:].indirect(lists["offs2"][:, entries]), seconds[half, t][:], ALU.subtract
                 )
-            for s in range(2):
-                for t in range(PACK):
+                for s in range(2):
                     nc.vector.tensor_scalar(
-                        scaled[s][:, t, :], raw[:, t, :], 0.0, factors[s][:, t : t + 1], ALU.max, ALU.mult
+                        scaled[:, s, t, :], raw[:, t, :], 0.0, factors[s][:, t : t + 1], ALU.max, ALU.mult
                     )
-            grouped = sb("table_grouped%d" % c, [P, 2, JC, PACK], BF16)
-            for s in range(2):
-                weave(nc.vector.tensor_copy, grouped[:, s, :, :], scaled[s][:])
-            table_codes[c] = sb("table_codes%d" % c, [P, 2 * JC], U32)
-            table_scales[c] = sb("table_scales%d" % c, [P, 2 * JC], U8)
-            nc.vector.quantize_mx(
-                table_codes[c][:].bitcast(FP8X4), table_scales[c][:], grouped[:].rearrange("p s j t -> p (s j t)")
+            return scaled
+
+        def quantise_table(name, scaled, grouped):
+            width = scaled.shape[3]
+            nc.vector.tensor_copy(
+                grouped.rearrange("p (s c i t) -> p s c t i", s=2, i=4, t=PACK),
+                scaled.rearrange("p s t (c i) -> p s c t i", i=4),
             )
+            codes = sb("table_codes" + name, [P, 2 * width], U32)
+            scales = sb("table_scales" + name, [P, 2 * width], U8)
+            nc.vector.quantize_mx(codes[:].bitcast(FP8X4), scales[:], grouped)
+            return codes, scales
 
         out_scales = sb("out_scales", [P, J], U8)
         out_rows = out_0.rearrange("(p r) j -> p r j", r=PACK)
         out_words = out_1[0].rearrange("p j t -> p (j t)").bitcast(I32)
 
-        def result(c, tag):
-            cols = slice(c * JC, (c + 1) * JC)
-            sums_sb = sb("result%d" % c, [P, PACK, JC], F32, tag)
-            per_bank = BANK // JC
-            for r0 in range(0, PACK, per_bank):
-                if r0 == 0:
-                    bank = turns.tile([P, BANK], F32, name="early_bank", tag="turned")
-                else:
-                    bank = sums.tile([P, BANK], F32, name="bank")
+        def result(name, cols, table, bank_tags, round_copy):
+            table_codes, table_scales = table
+            width = cols.stop - cols.start
+            sums_sb = sb("result" + name, [P, PACK, width], F32)
+            per_bank = BANK // width
+            for r0, tag in zip(range(0, PACK, per_bank), bank_tags):
+                pool = sums if tag == "bank" else turns
+                bank = pool.tile([P, BANK], F32, name="bank", tag=tag)
                 for r in range(r0, r0 + per_bank):
                     for s in range(2):
-                        e_cols = slice((2 * (r % 2) + s) * P, (2 * (r % 2) + s + 1) * P)
-                        j_cols = slice(s * JC, (s + 1) * JC)
+                        e_cols = slice(s * P, (s + 1) * P)
+                        j_cols = slice(s * width, (s + 1) * width)
                         nc.tensor.matmul_mx(
-                            bank[:, (r - r0) * JC : (r - r0 + 1) * JC],
-                            lhsT=value_codes[r // 2][:, e_cols].bitcast(FP8X4),
-                            lhsT_scale=value_scales[r // 2][:, e_cols],
-                            rhs=table_codes[c][:, j_cols].bitcast(FP8X4), rhs_scale=table_scales[c][:, j_cols],
+                            bank[:, (r - r0) * width : (r - r0 + 1) * width],
+                            lhsT=value_codes[r][:, e_cols].bitcast(FP8X4), lhsT_scale=value_scales[r][:, e_cols],
+                            rhs=table_codes[:, j_cols].bitcast(FP8X4), rhs_scale=table_scales[:, j_cols],
                             start=(s == 0), stop=(s == 1),
                         )
-                copy_out = nc.vector.tensor_copy if (c == CHUNKS - 1 and r0 > 0) else nc.scalar.copy
-                copy_out(sums_sb[:, r0 : r0 + per_bank, :].rearrange("p r j -> p (r j)"), bank[:])
+                nc.scalar.copy(sums_sb[:, r0 : r0 + per_bank, :].rearrange("p r j -> p (r j)"), bank[:])
             nc.sync.dma_start(out_rows[:, :, cols], sums_sb[:])
-            grouped = sb("result_grouped%d" % c, [P, JC, PACK], BF16)
-            weave(nc.vector.tensor_copy if c == CHUNKS - 1 else nc.scalar.copy, grouped[:], sums_sb[:])
-            codes = sb("result_codes%d" % c, [P, JC], U32)
-            nc.vector.quantize_mx(codes[:].bitcast(FP8X4), out_scales[:, cols], grouped[:].rearrange("p j r -> p (j r)"))
+            rounded = sb("result_grouped" + name, [P, width, PACK], BF16)
+            weave(round_copy, rounded[:], sums_sb[:])
+            codes = sb("result_codes" + name, [P, width], U32)
+            nc.vector.quantize_mx(codes[:].bitcast(FP8X4), out_scales[:, cols], rounded[:].rearrange("p j r -> p (j r)"))
             nc.sync.dma_start(out_words[:, cols], codes[:].bitcast(I32))
 
-        values(0, "vs", ("notes_grouped", "notes_codes1"))
-        look_up_second(0, "v")
-        table(0, None)
-        look_up_second(1, "s")
-        values(1, "ss", ("notes_scales1", "notes_codes1"))
-        table(1, "scaled0_0")
-        quantise_values(0, "second1")
-        values(2, "sv", ("notes_scales1", "table_grouped0"))
-        values(3, "ss", ("notes_scales1", "notes_codes1"))
-        quantise_values(1, "scaled0_1")
-        result(0, "notes_codes1")
-        result(1, None)
+        turned = [values(0, "vs", ("notes_grouped", "notes_codes1"))]
+        scaled0 = scaled_table(0, None, (None,) * PACK)
+        grouped0 = sb("table_grouped0", [P, 2 * HALF * PACK], BF16)
+        table0 = quantise_table("0", scaled0[:], grouped0[:])
+        for t in SCALAR_SECONDS:
+            look_up_second(1, t, "s", None)
+        turned.append(values(1, "ss", ("notes_scales1", None)))
+        leave_bank(0, turned[0], "plane0_1")
+        turned.append(values(2, "ss", (None, None)))
+        leave_bank(1, turned[1], "plane0_2")
+        turned.append(values(3, "ss", (None, None)))
+        leave_bank(2, turned[2], "plane0_3")
+        leave_bank(3, turned[3], None)
+        quantise_values(0, "table_grouped0")
+        scaled1 = scaled_table(1, "scaled0", ("raw0", "second0_3", "second0_2", "second0_1"))
+        quantise_values(1, "raw0")
+        quantise_values(2, QV2_TAG)
+        quantise_values(3, "scaled0")
+        result("0", slice(0, HALF), table0, ("turned0", "turned1"), nc.scalar.copy)
+        grouped1 = sb("table_grouped1", [P, 2, HALF * PACK], BF16, "values_grouped3")
+        for c in range(2):
+            table = quantise_table("1_%d" % c, scaled1[:, :, :, c * P : (c + 1) * P], grouped1[:, c, :])
+            result("1_%d" % c, slice(HALF + c * P, HALF + (c + 1) * P), table, ("bank",), nc.vector.tensor_copy)
         for q in range(4):
             queue = nc.sync if q % 2 == 0 else nc.scalar
             queue.dma_start(out_2[0, 4 * q : 4 * q + 4, :].bitcast(I32), out_scales[32 * q : 32 * q + 4, :].bitcast(I32))

@@ -18,10 +18,13 @@ D, T, I, J, U, E, Y = 512, 2048, 512, 512, 1024, 512, 1024
 P = 128
 PACK = 4
 BANK = 512
+QUADRANTS = 4
+PER_COLUMN = 16
+RUN = 4
 NOTE_HALVES = U // BANK
 HALF = J // 2
-SCALAR_SECONDS = (2, 3)
-QV2_TAG = "second1_2"
+SUM_BANKS = 6
+SCALAR_PLACES = (2, 3)
 SCALAR_NOTE_COLS = 256
 
 FLOPS = 2 * D * I * U + 2 * 2 * I * E * J
@@ -33,34 +36,33 @@ def tile_attend_tab_looked_twostores_pl_kernel(
     nc = tc.nc
     with ExitStack() as ctx:
         held = ctx.enter_context(tc.tile_pool(name="held", bufs=1))
-        sums = ctx.enter_context(tc.psum_pool(name="sums", bufs=6))
+        sums = ctx.enter_context(tc.psum_pool(name="sums", bufs=SUM_BANKS))
         turns = ctx.enter_context(tc.psum_pool(name="turns", bufs=1))
 
-        def sb(name, shape, dtype, tag=None):
-            return held.tile(shape, dtype, name=name, tag=tag or name, align_bytes=64)
+        def sb(name, shape, dtype, after=None):
+            return held.tile(shape, dtype, name=name, tag=after or name, align_bytes=64)
 
         def weave(engine_copy, dst, src):
-            engine_copy(dst.rearrange("p (c i) t -> p c t i", i=4), src.rearrange("p t (c i) -> p c t i", i=4))
+            engine_copy(dst.rearrange("p (c i) t -> p c t i", i=RUN), src.rearrange("p t (c i) -> p c t i", i=RUN))
 
-        def gather(engine, out, window):
-            if engine == "v":
-                nc.vector.tensor_copy(out, window)
-            else:
-                nc.scalar.activation(out, window, COPY)
+        def scalar_gather(out, window):
+            nc.scalar.activation(out, window, COPY)
+
+        vector_gather = nc.vector.tensor_copy
 
         lists = {}
         for name in ("offs", "offs2", "offs3", "offs4"):
-            lists[name] = held.tile([P, I // 16], U16, name="list_" + name)
+            lists[name] = held.tile([P, I // PER_COLUMN], U16, name="list_" + name)
         key_words = sb("key_words", [P, T], U16)
         key_scales = sb("key_scales", [P, T], U8)
         notes_raw = [sb("notes_raw%d" % h, [P, PACK, BANK], F32) for h in range(NOTE_HALVES)]
         stores = ((vals, T, "offs"), (vals2, Y, "offs4"))
-        planes = [[sb("plane%d_%d" % (s, r), [P, stores[s][1]], F32) for r in range(PACK)] for s in range(2)]
+        slabs = [[sb("slab%d_%d" % (s, r), [P, stores[s][1]], F32) for r in range(PACK)] for s in range(2)]
         factors = [sb("factor%d" % s, [P, PACK], F32) for s in range(2)]
 
         nc.gpsimd.memset(key_scales[:].bitcast(I32), 0)
         nc.sync.dma_start(lists["offs"][:], offs)
-        for q in range(4):
+        for q in range(QUADRANTS):
             nc.sync.dma_start(
                 key_scales[32 * q : 32 * q + 4, :].bitcast(I32), keys_scales[0, 4 * q : 4 * q + 4, :].bitcast(I32)
             )
@@ -74,112 +76,99 @@ def tile_attend_tab_looked_twostores_pl_kernel(
         for s, factor in enumerate((rowf, rowf2)):
             nc.sync.dma_start(factors[s][:], factor.rearrange("(p t) o -> p (t o)", t=PACK))
         for r in range(PACK):
-            for s in range(2):
-                nc.sync.dma_start(planes[s][r][:], stores[s][0].rearrange("(p r) c -> r p c", r=PACK)[r])
+            for s in (1, 0) if r == 0 else (0, 1):
+                nc.sync.dma_start(slabs[s][r][:], stores[s][0].rearrange("(p r) c -> r p c", r=PACK)[r])
         identity = sb("identity", [P, P], F32)
         make_identity(nc, identity[:])
 
         picked_words = sb("picked_words", [P, I], U16)
         dealt_words = sb("dealt_words", [P, I], U16)
         dealt_scales = sb("dealt_scales", [P, I], U8)
-        nc.vector.tensor_copy(
-            dealt_scales[:].rearrange("p (t m) -> p m t", t=PACK), key_scales[:].indirect(lists["offs"][:])
-        )
-        nc.vector.tensor_copy(picked_words[:], key_words[:].indirect(lists["offs"][:]))
+        vector_gather(dealt_scales[:].rearrange("p (t m) -> p m t", t=PACK), key_scales[:].indirect(lists["offs"][:]))
+        vector_gather(picked_words[:], key_words[:].indirect(lists["offs"][:]))
         nc.vector.tensor_copy(
             dealt_words[:].rearrange("p (t m) -> p t m", t=PACK), picked_words[:].rearrange("p (m t) -> p t m", t=PACK)
         )
 
         wide = [sb("wide%d" % t, [P, U], F32) for t in range(PACK)]
         for h in range(NOTE_HALVES):
-            grouped = sb("notes_grouped%d" % h, [P, BANK, PACK], BF16, "notes_grouped")
+            notes_woven = sb("notes_woven%d" % h, [P, BANK, PACK], BF16, after="notes_woven")
             cut = SCALAR_NOTE_COLS if h == 0 else 0
             if cut:
-                weave(nc.scalar.copy, grouped[:, :cut, :], notes_raw[h][:, :, :cut])
-            weave(nc.vector.tensor_copy, grouped[:, cut:, :], notes_raw[h][:, :, cut:])
-            codes = sb("notes_codes%d" % h, [P, BANK], U32)
-            scales = sb("notes_scales%d" % h, [P, BANK], U8)
-            nc.vector.quantize_mx(codes[:].bitcast(FP8X4), scales[:], grouped[:].rearrange("p u t -> p (u t)"))
+                weave(nc.scalar.copy, notes_woven[:, :cut, :], notes_raw[h][:, :, :cut])
+            weave(nc.vector.tensor_copy, notes_woven[:, cut:, :], notes_raw[h][:, :, cut:])
+            note_codes = sb("note_codes%d" % h, [P, BANK], U32)
+            note_scales = sb("note_scales%d" % h, [P, BANK], U8)
+            nc.vector.quantize_mx(
+                note_codes[:].bitcast(FP8X4), note_scales[:], notes_woven[:].rearrange("p u t -> p (u t)")
+            )
             for t in range(PACK):
-                cols = slice(t * P, (t + 1) * P)
+                rows = slice(t * P, (t + 1) * P)
                 bank = sums.tile([P, BANK], F32, name="bank")
                 nc.tensor.matmul_mx(
-                    bank[:], lhsT=dealt_words[:, cols].bitcast(FP4X4), lhsT_scale=dealt_scales[:, cols],
-                    rhs=codes[:].bitcast(FP8X4), rhs_scale=scales[:], start=True, stop=True,
+                    bank[:], lhsT=dealt_words[:, rows].bitcast(FP4X4), lhsT_scale=dealt_scales[:, rows],
+                    rhs=note_codes[:].bitcast(FP8X4), rhs_scale=note_scales[:], start=True, stop=True,
                 )
                 nc.scalar.copy(wide[t][:, h * BANK : (h + 1) * BANK], bank[:])
 
-        values_grouped, value_codes, value_scales = {}, {}, {}
+        values_woven, value_codes, value_scales = {}, {}, {}
 
-        def values(r, engines, tags):
+        def turn_values(r, gathers, after):
             turned = turns.tile([P, 2, 2, P], F32, name="turned", tag="turned%d" % (r % 2))
             for s in range(2):
-                picked = sb("picked%d_%d" % (s, r), [P, I], BF16, tags[s])
-                gather(engines[s], picked[:], planes[s][r][:].indirect(lists[stores[s][2]][:]))
+                picked = sb("picked%d_%d" % (s, r), [P, I], BF16, after[s])
+                gathers[s](picked[:], slabs[s][r][:].indirect(lists[stores[s][2]][:]))
                 pairs = picked[:].bitcast(F32)
                 for u in range(2):
                     nc.tensor.transpose(turned[:, s, u, :], pairs[:, u : I // 2 : 2], identity[:])
             return turned
 
-        def leave_bank(r, turned, tag):
-            values_grouped[r] = sb("values_grouped%d" % r, [P, 2 * P * PACK], BF16, tag)
+        def weave_values(r, turned, after):
+            values_woven[r] = sb("values_woven%d" % r, [P, 2 * P * PACK], BF16, after)
             nc.scalar.copy(
-                values_grouped[r][:].bitcast(F32).rearrange("p (s e u) -> p s e u", s=2, u=2),
+                values_woven[r][:].bitcast(F32).rearrange("p (s e u) -> p s e u", s=2, u=2),
                 turned[:].rearrange("p s u e -> p s e u"),
             )
 
-        def quantise_values(r, tag):
-            value_codes[r] = sb("values_codes%d" % r, [P, 2 * P], U32, tag)
-            value_scales[r] = sb("values_scales%d" % r, [P, 2 * P], U8)
-            nc.vector.quantize_mx(value_codes[r][:].bitcast(FP8X4), value_scales[r][:], values_grouped[r][:])
+        def quantise_values(r, after):
+            value_codes[r] = sb("value_codes%d" % r, [P, 2 * P], U32, after)
+            value_scales[r] = sb("value_scales%d" % r, [P, 2 * P], U8)
+            nc.vector.quantize_mx(value_codes[r][:].bitcast(FP8X4), value_scales[r][:], values_woven[r][:])
 
-        seconds = {}
+        def entries(name, half):
+            return lists[name][:, half * HALF // PER_COLUMN : (half + 1) * HALF // PER_COLUMN]
 
-        def look_up_second(half, t, engine, tag):
-            entries = slice(half * HALF // 16, (half + 1) * HALF // 16)
-            seconds[half, t] = sb("second%d_%d" % (half, t), [P, HALF], F32, tag)
-            gather(engine, seconds[half, t][:], wide[t][:].indirect(lists["offs3"][:, entries]))
+        def look_up_subtrahend(gather, out, half, t):
+            gather(out, wide[t][:].indirect(entries("offs3", half)))
 
-        def scaled_table(half, raw_tag, second_tags):
-            entries = slice(half * HALF // 16, (half + 1) * HALF // 16)
-            raw = sb("raw%d" % half, [P, PACK, HALF], F32, raw_tag)
-            scaled = sb("scaled%d" % half, [P, 2, PACK, HALF], BF16)
-            for t in range(PACK):
-                if (half, t) not in seconds:
-                    look_up_second(half, t, "v", second_tags[t])
-                nc.vector.tensor_tensor(
-                    raw[:, t, :], wide[t][:].indirect(lists["offs2"][:, entries]), seconds[half, t][:], ALU.subtract
-                )
-                for s in range(2):
-                    nc.vector.tensor_scalar(
-                        scaled[:, s, t, :], raw[:, t, :], 0.0, factors[s][:, t : t + 1], ALU.max, ALU.mult
-                    )
-            return scaled
+        def scale_piece(scaled, raw, subtrahend, half, t):
+            nc.vector.tensor_tensor(raw[:], wide[t][:].indirect(entries("offs2", half)), subtrahend, ALU.subtract)
+            for s in range(2):
+                nc.vector.tensor_scalar(scaled[:, s, t, :], raw[:], 0.0, factors[s][:, t : t + 1], ALU.max, ALU.mult)
 
-        def quantise_table(name, scaled, grouped):
+        def quantise_table(name, scaled, woven):
             width = scaled.shape[3]
             nc.vector.tensor_copy(
-                grouped.rearrange("p (s c i t) -> p s c t i", s=2, i=4, t=PACK),
-                scaled.rearrange("p s t (c i) -> p s c t i", i=4),
+                woven.rearrange("p (s c i t) -> p s c t i", s=2, i=RUN, t=PACK),
+                scaled.rearrange("p s t (c i) -> p s c t i", i=RUN),
             )
             codes = sb("table_codes" + name, [P, 2 * width], U32)
             scales = sb("table_scales" + name, [P, 2 * width], U8)
-            nc.vector.quantize_mx(codes[:].bitcast(FP8X4), scales[:], grouped)
+            nc.vector.quantize_mx(codes[:].bitcast(FP8X4), scales[:], woven)
             return codes, scales
 
         out_scales = sb("out_scales", [P, J], U8)
         out_rows = out_0.rearrange("(p r) j -> p r j", r=PACK)
         out_words = out_1[0].rearrange("p j t -> p (j t)").bitcast(I32)
 
-        def result(name, cols, table, bank_tags, round_copy):
+        def multiply(name, cols, table, banks, after=None):
             table_codes, table_scales = table
             width = cols.stop - cols.start
-            sums_sb = sb("result" + name, [P, PACK, width], F32)
+            result = sb("result" + name, [P, PACK, width], F32, after)
             per_bank = BANK // width
-            for r0, tag in zip(range(0, PACK, per_bank), bank_tags):
-                pool = sums if tag == "bank" else turns
+            for r0, (pool, tag) in zip(range(0, PACK, per_bank), banks):
                 bank = pool.tile([P, BANK], F32, name="bank", tag=tag)
-                for r in range(r0, r0 + per_bank):
+                for r in reversed(range(r0, r0 + per_bank)):
                     for s in range(2):
                         e_cols = slice(s * P, (s + 1) * P)
                         j_cols = slice(s * width, (s + 1) * width)
@@ -189,37 +178,71 @@ def tile_attend_tab_looked_twostores_pl_kernel(
                             rhs=table_codes[:, j_cols].bitcast(FP8X4), rhs_scale=table_scales[:, j_cols],
                             start=(s == 0), stop=(s == 1),
                         )
-                nc.scalar.copy(sums_sb[:, r0 : r0 + per_bank, :].rearrange("p r j -> p (r j)"), bank[:])
-            nc.sync.dma_start(out_rows[:, :, cols], sums_sb[:])
-            rounded = sb("result_grouped" + name, [P, width, PACK], BF16)
-            weave(round_copy, rounded[:], sums_sb[:])
-            codes = sb("result_codes" + name, [P, width], U32)
+                nc.scalar.copy(result[:, r0 : r0 + per_bank, :].rearrange("p r j -> p (r j)"), bank[:])
+            nc.sync.dma_start(out_rows[:, :, cols], result[:])
+            return result
+
+        def round_result(quarter, engine_copy, result, after=None):
+            rounded = sb("rounded%d" % quarter, [P, P, PACK], BF16, after)
+            weave(engine_copy, rounded[:], result)
+            return rounded
+
+        def store_planes(quarter, rounded, after=None):
+            cols = slice(quarter * P, (quarter + 1) * P)
+            codes = sb("result_codes%d" % quarter, [P, P], U32, after)
             nc.vector.quantize_mx(codes[:].bitcast(FP8X4), out_scales[:, cols], rounded[:].rearrange("p j r -> p (j r)"))
             nc.sync.dma_start(out_words[:, cols], codes[:].bitcast(I32))
 
-        turned = [values(0, "vs", ("notes_grouped", "notes_codes1"))]
-        scaled0 = scaled_table(0, None, (None,) * PACK)
-        grouped0 = sb("table_grouped0", [P, 2 * HALF * PACK], BF16)
-        table0 = quantise_table("0", scaled0[:], grouped0[:])
-        for t in SCALAR_SECONDS:
-            look_up_second(1, t, "s", None)
-        turned.append(values(1, "ss", ("notes_scales1", None)))
-        leave_bank(0, turned[0], "plane0_1")
-        turned.append(values(2, "ss", (None, None)))
-        leave_bank(1, turned[1], "plane0_2")
-        turned.append(values(3, "ss", (None, None)))
-        leave_bank(2, turned[2], "plane0_3")
-        leave_bank(3, turned[3], None)
-        quantise_values(0, "table_grouped0")
-        scaled1 = scaled_table(1, "scaled0", ("raw0", "second0_3", "second0_2", "second0_1"))
-        quantise_values(1, "raw0")
-        quantise_values(2, QV2_TAG)
-        quantise_values(3, "scaled0")
-        result("0", slice(0, HALF), table0, ("turned0", "turned1"), nc.scalar.copy)
-        grouped1 = sb("table_grouped1", [P, 2, HALF * PACK], BF16, "values_grouped3")
+        turned = [turn_values(0, (scalar_gather, vector_gather), after=("note_codes1", "notes_woven"))]
+
+        subtrahends0 = sb("subtrahends0", [P, PACK, HALF], F32, after="slab1_0")
+        scaled0 = sb("scaled0", [P, 2, PACK, HALF], BF16)
+        for t in range(PACK):
+            raw = sb("raw0_%d" % t, [P, HALF], F32)
+            look_up_subtrahend(vector_gather, subtrahends0[:, t, :], 0, t)
+            scale_piece(scaled0, raw, subtrahends0[:, t, :], 0, t)
+        table_woven0 = sb("table_woven0", [P, 2 * HALF * PACK], BF16)
+        table0 = quantise_table("0", scaled0[:], table_woven0[:])
+
+        subtrahends1 = {}
+        for t in SCALAR_PLACES:
+            subtrahends1[t] = sb("subtrahend1_%d" % t, [P, HALF], F32)
+            look_up_subtrahend(scalar_gather, subtrahends1[t][:], 1, t)
+        for r in range(1, PACK):
+            behind_g1 = "note_scales1" if r == 1 else None
+            turned.append(turn_values(r, (scalar_gather, scalar_gather), after=(behind_g1, None)))
+            weave_values(r - 1, turned[r - 1], after="slab0_%d" % r)
+        weave_values(PACK - 1, turned[PACK - 1], after=None)
+
+        quantise_values(0, after="table_woven0")
+        slab_before_piece = {1: 1, 3: 2}
+        raw_after = ("scaled0", "slab0_2", "slab1_0", "slab0_3")
+        scaled1 = sb("scaled1", [P, 2, PACK, HALF], BF16)
+        for t in range(PACK):
+            if t in slab_before_piece:
+                quantise_values(slab_before_piece[t], after="subtrahend1_%d" % (t - 1))
+            raw = sb("raw1_%d" % t, [P, HALF], F32, after=raw_after[t])
+            if t not in SCALAR_PLACES:
+                subtrahends1[t] = sb("subtrahend1_%d" % t, [P, HALF], F32)
+                look_up_subtrahend(vector_gather, subtrahends1[t][:], 1, t)
+            scale_piece(scaled1, raw, subtrahends1[t][:], 1, t)
+        quantise_values(PACK - 1, after="subtrahend1_%d" % (PACK - 1))
+
+        result0 = multiply("0", slice(0, HALF), table0, ((turns, "turned0"), (turns, "turned1")), after="slab1_3")
+        rounded0 = round_result(0, nc.scalar.copy, result0[:, :, :P])
+
+        table_woven1 = sb("table_woven1", [P, 2, HALF * PACK], BF16, after="values_woven3")
+        late_results = []
         for c in range(2):
-            table = quantise_table("1_%d" % c, scaled1[:, :, :, c * P : (c + 1) * P], grouped1[:, c, :])
-            result("1_%d" % c, slice(HALF + c * P, HALF + (c + 1) * P), table, ("bank",), nc.vector.tensor_copy)
-        for q in range(4):
+            table = quantise_table("1_%d" % c, scaled1[:, :, :, c * P : (c + 1) * P], table_woven1[:, c, :])
+            cols = slice(HALF + c * P, HALF + (c + 1) * P)
+            late_results.append(multiply("1_%d" % c, cols, table, ((sums, "bank"),)))
+
+        rounded1 = round_result(1, nc.vector.tensor_copy, result0[:, :, P:], after="values_woven3")
+        store_planes(0, rounded0, after="scaled1")
+        store_planes(1, rounded1)
+        for c in range(2):
+            store_planes(2 + c, round_result(2 + c, nc.vector.tensor_copy, late_results[c][:]))
+        for q in range(QUADRANTS):
             queue = nc.sync if q % 2 == 0 else nc.scalar
             queue.dma_start(out_2[0, 4 * q : 4 * q + 4, :].bitcast(I32), out_scales[32 * q : 32 * q + 4, :].bitcast(I32))

from contextlib import ExitStack

import concourse.mybir as mybir
from concourse.masks import make_identity

F32 = mybir.dt.float32
BF16 = mybir.dt.bfloat16
I32 = mybir.dt.int32
U32 = mybir.dt.uint32
U16 = mybir.dt.uint16
U8 = mybir.dt.uint8
FP8X4 = mybir.dt.float8_e4m3fn_x4
FP4X4 = mybir.dt.float4_e2m1fn_x4
COPY = mybir.ActivationFunctionType.Copy
ALU = mybir.AluOpType

D, T, I, J, U, E, Y = 512, 2048, 512, 512, 1024, 512, 1024
P = 128
PACK = 4
BANK = 512
QUADRANTS = 4
PER_COLUMN = 16
RUN = 4
NOTE_HALVES = U // BANK
HALF = J // 2
SUM_BANKS = 6
SCALAR_PLACES = (2, 3)
SCALAR_NOTE_COLS = 256

FLOPS = 2 * D * I * U + 2 * 2 * I * E * J


def tile_attend_tab_looked_twostores_pl_kernel(
    tc, keys_words, keys_scales, notes, rowf, rowf2, vals, vals2, offs, offs2, offs3, offs4, out_0, out_1, out_2
):
    nc = tc.nc
    with ExitStack() as ctx:
        held = ctx.enter_context(tc.tile_pool(name="held", bufs=1))
        sums = ctx.enter_context(tc.psum_pool(name="sums", bufs=SUM_BANKS))
        turns = ctx.enter_context(tc.psum_pool(name="turns", bufs=1))

        def sb(name, shape, dtype, after=None):
            return held.tile(shape, dtype, name=name, tag=after or name, align_bytes=64)

        def weave(engine_copy, dst, src):
            engine_copy(dst.rearrange("p (c i) t -> p c t i", i=RUN), src.rearrange("p t (c i) -> p c t i", i=RUN))

        def scalar_gather(out, window):
            nc.scalar.activation(out, window, COPY)

        vector_gather = nc.vector.tensor_copy

        lists = {}
        for name in ("offs", "offs2", "offs3", "offs4"):
            lists[name] = held.tile([P, I // PER_COLUMN], U16, name="list_" + name)
        key_words = sb("key_words", [P, T], U16)
        key_scales = sb("key_scales", [P, T], U8)
        notes_raw = [sb("notes_raw%d" % h, [P, PACK, BANK], F32) for h in range(NOTE_HALVES)]
        stores = ((vals, T, "offs"), (vals2, Y, "offs4"))
        slabs = [[sb("slab%d_%d" % (s, r), [P, stores[s][1]], F32) for r in range(PACK)] for s in range(2)]
        factors = [sb("factor%d" % s, [P, PACK], F32) for s in range(2)]

        nc.gpsimd.memset(key_scales[:].bitcast(I32), 0)
        nc.sync.dma_start(lists["offs"][:], offs)
        for q in range(QUADRANTS):
            nc.sync.dma_start(
                key_scales[32 * q : 32 * q + 4, :].bitcast(I32), keys_scales[0, 4 * q : 4 * q + 4, :].bitcast(I32)
            )
        nc.sync.dma_start(key_words[:].bitcast(I32), keys_words[0].bitcast(I32))
        notes_rows = notes.rearrange("(p t) u -> p t u", t=PACK)
        for h in range(NOTE_HALVES):
            nc.sync.dma_start(notes_raw[h][:], notes_rows[:, :, h * BANK : (h + 1) * BANK])
        nc.sync.dma_start(lists["offs4"][:], offs4)
        nc.sync.dma_start(lists["offs3"][:], offs3)
        nc.sync.dma_start(lists["offs2"][:], offs2)
        for s, factor in enumerate((rowf, rowf2)):
            nc.sync.dma_start(factors[s][:], factor.rearrange("(p t) o -> p (t o)", t=PACK))
        for r in range(PACK):
            for s in (1, 0) if r == 0 else (0, 1):
                nc.sync.dma_start(slabs[s][r][:], stores[s][0].rearrange("(p r) c -> r p c", r=PACK)[r])
        identity = sb("identity", [P, P], F32)
        make_identity(nc, identity[:])

        picked_words = sb("picked_words", [P, I], U16)
        dealt_words = sb("dealt_words", [P, I], U16)
        dealt_scales = sb("dealt_scales", [P, I], U8)
        vector_gather(dealt_scales[:].rearrange("p (t m) -> p m t", t=PACK), key_scales[:].indirect(lists["offs"][:]))
        vector_gather(picked_words[:], key_words[:].indirect(lists["offs"][:]))
        nc.vector.tensor_copy(
            dealt_words[:].rearrange("p (t m) -> p t m", t=PACK), picked_words[:].rearrange("p (m t) -> p t m", t=PACK)
        )

        wide = [sb("wide%d" % t, [P, U], F32) for t in range(PACK)]
        for h in range(NOTE_HALVES):
            notes_woven = sb("notes_woven%d" % h, [P, BANK, PACK], BF16, after="notes_woven")
            cut = SCALAR_NOTE_COLS if h == 0 else 0
            if cut:
                weave(nc.scalar.copy, notes_woven[:, :cut, :], notes_raw[h][:, :, :cut])
            weave(nc.vector.tensor_copy, notes_woven[:, cut:, :], notes_raw[h][:, :, cut:])
            note_codes = sb("note_codes%d" % h, [P, BANK], U32)
            note_scales = sb("note_scales%d" % h, [P, BANK], U8)
            nc.vector.quantize_mx(
                note_codes[:].bitcast(FP8X4), note_scales[:], notes_woven[:].rearrange("p u t -> p (u t)")
            )
            for t in range(PACK):
                rows = slice(t * P, (t + 1) * P)
                bank = sums.tile([P, BANK], F32, name="bank")
                nc.tensor.matmul_mx(
                    bank[:], lhsT=dealt_words[:, rows].bitcast(FP4X4), lhsT_scale=dealt_scales[:, rows],
                    rhs=note_codes[:].bitcast(FP8X4), rhs_scale=note_scales[:], start=True, stop=True,
                )
                nc.scalar.copy(wide[t][:, h * BANK : (h + 1) * BANK], bank[:])

        values_woven, value_codes, value_scales = {}, {}, {}

        def turn_values(r, gathers, after):
            turned = turns.tile([P, 2, 2, P], F32, name="turned", tag="turned%d" % (r % 2))
            for s in range(2):
                picked = sb("picked%d_%d" % (s, r), [P, I], BF16, after[s])
                gathers[s](picked[:], slabs[s][r][:].indirect(lists[stores[s][2]][:]))
                pairs = picked[:].bitcast(F32)
                for u in range(2):
                    nc.tensor.transpose(turned[:, s, u, :], pairs[:, u : I // 2 : 2], identity[:])
            return turned

        def weave_values(r, turned, after):
            values_woven[r] = sb("values_woven%d" % r, [P, 2 * P * PACK], BF16, after)
            nc.scalar.copy(
                values_woven[r][:].bitcast(F32).rearrange("p (s e u) -> p s e u", s=2, u=2),
                turned[:].rearrange("p s u e -> p s e u"),
            )

        def quantise_values(r, after):
            value_codes[r] = sb("value_codes%d" % r, [P, 2 * P], U32, after)
            value_scales[r] = sb("value_scales%d" % r, [P, 2 * P], U8)
            nc.vector.quantize_mx(value_codes[r][:].bitcast(FP8X4), value_scales[r][:], values_woven[r][:])

        def entries(name, half):
            return lists[name][:, half * HALF // PER_COLUMN : (half + 1) * HALF // PER_COLUMN]

        def look_up_subtrahend(gather, out, half, t):
            gather(out, wide[t][:].indirect(entries("offs3", half)))

        def scale_piece(scaled, raw, subtrahend, half, t):
            nc.vector.tensor_tensor(raw[:], wide[t][:].indirect(entries("offs2", half)), subtrahend, ALU.subtract)
            for s in range(2):
                nc.vector.tensor_scalar(scaled[:, s, t, :], raw[:], 0.0, factors[s][:, t : t + 1], ALU.max, ALU.mult)

        def quantise_table(name, scaled, woven):
            width = scaled.shape[3]
            nc.vector.tensor_copy(
                woven.rearrange("p (s c i t) -> p s c t i", s=2, i=RUN, t=PACK),
                scaled.rearrange("p s t (c i) -> p s c t i", i=RUN),
            )
            codes = sb("table_codes" + name, [P, 2 * width], U32)
            scales = sb("table_scales" + name, [P, 2 * width], U8)
            nc.vector.quantize_mx(codes[:].bitcast(FP8X4), scales[:], woven)
            return codes, scales

        out_scales = sb("out_scales", [P, J], U8)
        out_rows = out_0.rearrange("(p r) j -> p r j", r=PACK)
        out_words = out_1[0].rearrange("p j t -> p (j t)").bitcast(I32)

        def multiply(name, cols, table, banks, after=None):
            table_codes, table_scales = table
            width = cols.stop - cols.start
            result = sb("result" + name, [P, PACK, width], F32, after)
            per_bank = BANK // width
            for r0, (pool, tag) in zip(range(0, PACK, per_bank), banks):
                bank = pool.tile([P, BANK], F32, name="bank", tag=tag)
                for r in reversed(range(r0, r0 + per_bank)):
                    for s in range(2):
                        e_cols = slice(s * P, (s + 1) * P)
                        j_cols = slice(s * width, (s + 1) * width)
                        nc.tensor.matmul_mx(
                            bank[:, (r - r0) * width : (r - r0 + 1) * width],
                            lhsT=value_codes[r][:, e_cols].bitcast(FP8X4), lhsT_scale=value_scales[r][:, e_cols],
                            rhs=table_codes[:, j_cols].bitcast(FP8X4), rhs_scale=table_scales[:, j_cols],
                            start=(s == 0), stop=(s == 1),
                        )
                nc.scalar.copy(result[:, r0 : r0 + per_bank, :].rearrange("p r j -> p (r j)"), bank[:])
            nc.sync.dma_start(out_rows[:, :, cols], result[:])
            return result

        def round_result(quarter, engine_copy, result, after=None):
            rounded = sb("rounded%d" % quarter, [P, P, PACK], BF16, after)
            weave(engine_copy, rounded[:], result)
            return rounded

        def store_planes(quarter, rounded, after=None):
            cols = slice(quarter * P, (quarter + 1) * P)
            codes = sb("result_codes%d" % quarter, [P, P], U32, after)
            nc.vector.quantize_mx(codes[:].bitcast(FP8X4), out_scales[:, cols], rounded[:].rearrange("p j r -> p (j r)"))
            nc.sync.dma_start(out_words[:, cols], codes[:].bitcast(I32))

        turned = [turn_values(0, (scalar_gather, vector_gather), after=("note_codes1", "notes_woven"))]

        subtrahends0 = sb("subtrahends0", [P, PACK, HALF], F32, after="slab1_0")
        scaled0 = sb("scaled0", [P, 2, PACK, HALF], BF16)
        for t in range(PACK):
            raw = sb("raw0_%d" % t, [P, HALF], F32)
            look_up_subtrahend(vector_gather, subtrahends0[:, t, :], 0, t)
            scale_piece(scaled0, raw, subtrahends0[:, t, :], 0, t)
        table_woven0 = sb("table_woven0", [P, 2 * HALF * PACK], BF16)
        table0 = quantise_table("0", scaled0[:], table_woven0[:])

        subtrahends1 = {}
        for t in SCALAR_PLACES:
            subtrahends1[t] = sb("subtrahend1_%d" % t, [P, HALF], F32)
            look_up_subtrahend(scalar_gather, subtrahends1[t][:], 1, t)
        for r in range(1, PACK):
            behind_g1 = "note_scales1" if r == 1 else None
            turned.append(turn_values(r, (scalar_gather, scalar_gather), after=(behind_g1, None)))
            weave_values(r - 1, turned[r - 1], after="slab0_%d" % r)
        weave_values(PACK - 1, turned[PACK - 1], after=None)

        quantise_values(0, after="table_woven0")
        slab_before_piece = {1: 1, 3: 2}
        raw_after = ("scaled0", "slab0_2", "slab1_0", "slab0_3")
        scaled1 = sb("scaled1", [P, 2, PACK, HALF], BF16)
        for t in range(PACK):
            if t in slab_before_piece:
                quantise_values(slab_before_piece[t], after="subtrahend1_%d" % (t - 1))
            raw = sb("raw1_%d" % t, [P, HALF], F32, after=raw_after[t])
            if t not in SCALAR_PLACES:
                subtrahends1[t] = sb("subtrahend1_%d" % t, [P, HALF], F32)
                look_up_subtrahend(vector_gather, subtrahends1[t][:], 1, t)
            scale_piece(scaled1, raw, subtrahends1[t][:], 1, t)
        quantise_values(PACK - 1, after="subtrahend1_%d" % (PACK - 1))

        result0 = multiply("0", slice(0, HALF), table0, ((turns, "turned0"), (turns, "turned1")), after="slab1_3")
        rounded0 = round_result(0, nc.scalar.copy, result0[:, :, :P])

        table_woven1 = sb("table_woven1", [P, 2, HALF * PACK], BF16, after="values_woven3")
        late_results = []
        for c in range(2):
            table = quantise_table("1_%d" % c, scaled1[:, :, :, c * P : (c + 1) * P], table_woven1[:, c, :])
            cols = slice(HALF + c * P, HALF + (c + 1) * P)
            late_results.append(multiply("1_%d" % c, cols, table, ((sums, "bank"),)))

        rounded1 = round_result(1, nc.vector.tensor_copy, result0[:, :, P:], after="values_woven3")
        store_planes(0, rounded0, after="scaled1")
        store_planes(1, rounded1)
        for c in range(2):
            store_planes(2 + c, round_result(2 + c, nc.vector.tensor_copy, late_results[c][:]))
        for q in range(QUADRANTS):
            queue = nc.sync if q % 2 == 0 else nc.scalar
            queue.dma_start(out_2[0, 4 * q : 4 * q + 4, :].bitcast(I32), out_scales[32 * q : 32 * q + 4, :].bitcast(I32))
